import numpy as np
import ml_dtypes


def mxq(x, axis, fmt="e4m3"):
    dtype, down = {"e4m3": (ml_dtypes.float8_e4m3fn, 7), "e5m2": (ml_dtypes.float8_e5m2, 14)}[fmt]
    v = np.moveaxis(np.asarray(x, np.float32).astype(ml_dtypes.bfloat16).astype(np.float64), axis, -1)
    blocks = v.reshape(v.shape[:-1] + (-1, 32))
    amax = np.abs(blocks).max(-1, keepdims=True)
    byte = np.maximum(np.where(amax > 0, np.frexp(amax)[1] - 1 + 127, 0) - down, 1)
    scale = np.exp2(byte - 127.0)
    codes = (blocks / scale).astype(np.float32).astype(dtype).astype(np.float64)
    return np.moveaxis((codes * scale).reshape(v.shape), -1, axis)


WIDE = False


def mx_kscale(k):
    if not WIDE:
        return np.ones(k)
    levels = np.array([10, -10, 5, -5, 0])
    if k % 512:
        return np.exp2(np.random.permutation(np.resize(levels, k // 32))).repeat(32)
    a = np.empty((k // 512, 16))
    for p in range(k // 512):
        a[p, :8] = np.random.permutation(np.resize(levels, 8))
        for g in range(8):
            far = levels[np.abs(levels - a[p, g]) >= 10]
            a[p, g + 8] = far[np.random.randint(len(far))]
    return np.exp2(a.ravel()).repeat(32)


def f64(x):
    return np.asarray(x).astype(np.float64)


def striped(idx):
    return np.tile(np.asarray(idx).reshape(-1, 16).T, (8, 1)).astype(np.uint16)


def unstriped(offs):
    return offs[:16].T.reshape(-1).astype(np.int64)


E2M1 = np.array([0.0, 0.5, 1.0, 1.5, 2.0, 3.0, 4.0, 6.0, -0.0, -0.5, -1.0, -1.5, -2.0, -3.0, -4.0, -6.0])


def pack_weight(w, fmt):
    k, n = w.shape
    w = f64(np.asarray(w, np.float32).astype(ml_dtypes.bfloat16)).reshape(k // 32, 32, n)
    amax = np.abs(w).max(1)
    if fmt == "e4m3":
        byte = np.frexp(amax)[1] - 1 + 127 - 7
    else:
        mant, ex = np.frexp(amax / 6.0)
        byte = np.where(mant > 0.5, ex, ex - 1) + 127
    byte = np.clip(np.where(amax > 0, byte, 1), 1, 254)
    scaled = (w * np.exp2(127.0 - byte)[:, None, :]).reshape(k, n).astype(np.float32)
    by_word = np.ascontiguousarray(scaled.reshape(k // 512, 128, 4, n).transpose(0, 1, 3, 2))
    if fmt == "e4m3":
        words = by_word.astype(ml_dtypes.float8_e4m3fn).view(np.uint8)
    else:
        c = by_word.astype(ml_dtypes.float4_e2m1fn).view(np.uint8) & 0xF
        words = (c[..., 0::2] | (c[..., 1::2] << 4)).reshape(k // 512, 128, 2 * n)
    return np.ascontiguousarray(words), np.ascontiguousarray(byte.astype(np.uint8).reshape(k // 512, 16, n))


def unpack_weight(words, scales, fmt):
    g, _, n = scales.shape
    words = np.ascontiguousarray(words).reshape(g, 128, n, -1)
    if fmt == "e4m3":
        vals = words.view(ml_dtypes.float8_e4m3fn).astype(np.float64)
    else:
        nib = np.empty((g, 128, n, 4), np.uint8)
        nib[..., 0::2] = words & 0xF
        nib[..., 1::2] = words >> 4
        vals = E2M1[nib]
    vals = vals * np.repeat(np.exp2(scales.astype(np.float64) - 127.0), 8, axis=1)[..., None]
    return vals.transpose(0, 1, 3, 2).reshape(g * 512, n)


D, K, V, I, T, Q = 512, 512, 1024, 512, 2048, 128


def setup_inputs():
    n = np.random.standard_normal
    idx = np.random.permutation(T)[:I]
    idx2 = np.random.permutation(V)[:I]
    fd = mx_kscale(D)
    fk = mx_kscale(K)
    embp = pack_weight(n((K, T)) / fk[:, None], "e4m3")
    return {
        "ht": (n((D, Q)) * 1.0 / np.sqrt(D) * fd[:, None]).astype(np.float32),
        "hd": (n((K, Q)) * 1.0 / np.sqrt(K) * fk[:, None]).astype(np.float32),
        "voc": (n((D, V)) / fd[:, None]).astype(np.float32),
        "emb_words": embp[0],
        "emb_scales": embp[1],
        "dw": (np.random.uniform(0.3, 0.7, (Q, 1))).astype(np.float32),
        "offs": striped(idx),
        "offs2": striped(idx2),
    }


def reference(ht, hd, voc, emb_words, emb_scales, dw, offs, offs2):
    idx = unstriped(offs)
    idx2 = unstriped(offs2)
    embu = unpack_weight(emb_words, emb_scales, "e4m3")
    htq = mxq(f64(ht), 0, "e4m3")
    vocq = mxq(f64(voc), 0, "e4m3")
    a = htq.T @ vocq
    hdq = mxq(f64(hd), 0, "e4m3")
    embidxg = embu[:, idx]
    b = hdq.T @ embidxg
    m1 = np.max(a, axis=1, keepdims=True)
    z = np.sum(np.exp(a - m1), axis=1, keepdims=True)
    r = np.exp(b - np.max(b, axis=1, keepdims=True))
    u = np.minimum(np.exp(a[:, idx2] - m1) / z, r * f64(dw) / np.sum(r, axis=1, keepdims=True))
    y = u / np.sum(u, axis=1, keepdims=True) * 512.0
    return y

@@ -1,0 +1,177 @@
+from contextlib import ExitStack
+
+import concourse.mybir as mybir
+
+F32 = mybir.dt.float32
+BF16 = mybir.dt.bfloat16
+I32 = mybir.dt.int32
+U32 = mybir.dt.uint32
+U16 = mybir.dt.uint16
+U8 = mybir.dt.uint8
+FP8X4 = mybir.dt.float8_e4m3fn_x4
+ALU = mybir.AluOpType
+ACT = mybir.ActivationFunctionType
+
+P = 128
+PACK = 4
+D, V, I, T, Q = 512, 1024, 512, 2048, 128
+CHUNK = 256
+HALF = I // 2
+SCALAR_COLS = [160, 160, 160, 96]
+BANKS = [[0], [1], [2], [3]]
+FLOPS = 2 * D * Q * (V + I)
+
+
+def interleave(engine_copy, grouped, raw, c0, c1):
+    engine_copy(
+        out=grouped[:, c0:c1, :].rearrange("p (c i) t -> p c t i", i=4),
+        in_=raw[:, :, c0:c1].rearrange("p t (c i) -> p c t i", i=4),
+    )
+
+
+def tile_attend_acceptedmass_kernel(tc, ht, hd, voc, emb_words, emb_scales, dw, offs, offs2, out):
+    nc = tc.nc
+    n_chunks = V // CHUNK
+    with ExitStack() as ctx:
+        sb = ctx.enter_context(tc.tile_pool(name="sb", bufs=1))
+        late = ctx.enter_context(tc.tile_pool(name="late", bufs=1))
+        ps = ctx.enter_context(tc.psum_pool(name="ps", bufs=1))
+
+        offs_sb = sb.tile([P, I // 16], U16, name="offs_sb")
+        offs2_sb = sb.tile([P, I // 16], U16, name="offs2_sb")
+        scale_store = sb.tile([P, T], U8, name="scale_store", tag="scales_then_codes", align_bytes=64)
+        ht_raw = sb.tile([P, PACK, Q], F32, name="ht_raw")
+        chunk_bytes = PACK * CHUNK * 4
+        late_bytes = 4 * chunk_bytes + PACK * Q * 4 + T * 4 + 32
+        gate = late.tile([P, late_bytes // 4], F32, name="gate", offset=0)
+        voc_raw = [late.tile([P, PACK, CHUNK], F32, name=f"voc_raw{c}", offset=c * chunk_bytes) for c in range(n_chunks)]
+        hd_raw = late.tile([P, PACK, Q], F32, name="hd_raw", offset=4 * chunk_bytes)
+        store_offset = 4 * chunk_bytes + PACK * Q * 4
+        word_store = late.tile([P, T], U32, name="word_store", offset=store_offset)
+
+        dw_sb = late.tile([P, 1], F32, name="dw_sb", offset=store_offset + T * 4)
+        warm = sb.tile([P, 1], F32, name="warm")
+        warm_out = sb.tile([P, 1], F32, name="warm_out")
+        nc.vector.memset(scale_store[:].bitcast(U32), 0)
+        nc.vector.memset(gate[:, 0:1], 0.0)
+        nc.vector.tensor_copy(warm[:], gate[:, 0:1])
+        nc.scalar.activation(warm_out[:], warm[:], ACT.Exp)
+        a_sb = sb.tile([P, V], F32, name="a_sb", tag="a_then_words", align_bytes=64)
+
+        voc_v = voc.rearrange("(p j) w -> p j w", j=PACK)
+        nc.sync.dma_start(offs_sb[:], offs)
+        nc.sync.dma_start(out=ht_raw[:], in_=ht.rearrange("(p j) w -> p j w", j=PACK))
+        for g in range(4):
+            nc.sync.dma_start(
+                out=scale_store[32 * g : 32 * g + 4, :].bitcast(I32),
+                in_=emb_scales[0, 4 * g : 4 * g + 4, :].bitcast(I32),
+            )
+        for c in range(n_chunks):
+            nc.sync.dma_start(out=voc_raw[c][:], in_=voc_v[:, :, c * CHUNK : (c + 1) * CHUNK])
+        nc.sync.dma_start(out=hd_raw[:], in_=hd.rearrange("(p j) w -> p j w", j=PACK))
+        nc.sync.dma_start(out=dw_sb[:], in_=dw)
+        nc.sync.dma_start(
+            out=word_store[:].bitcast(I32),
+            in_=emb_words[0].rearrange("p n t -> p (n t)").bitcast(I32),
+        )
+
+        nc.sync.dma_start(offs2_sb[:], offs2)
+
+        def quantize(name, grouped, width):
+            tag = "scales_then_codes" if name == "voc0" else name + "_codes"
+            codes = sb.tile([P, width], U32, name=name + "_codes", tag=tag, align_bytes=64)
+            scales = sb.tile([P, width], U8, name=name + "_scales", align_bytes=64)
+            nc.vector.quantize_mx(
+                out=codes[:].bitcast(FP8X4), scales=scales[:], in_=grouped[:].rearrange("p w j -> p (w j)")
+            )
+            return codes, scales
+
+        ht_grouped = sb.tile([P, Q, PACK], BF16, name="ht_grouped", align_bytes=64)
+        interleave(nc.scalar.copy, ht_grouped, ht_raw, 0, Q)
+        ht_codes, ht_scales = quantize("ht", ht_grouped, Q)
+        emb_scale_g = sb.tile([P, I], U8, name="emb_scale_g", align_bytes=64)
+        nc.vector.tensor_copy(emb_scale_g[:], scale_store[:].indirect(offs_sb[:]))
+
+        a_max = []
+        a_ps = [ps.tile([P, CHUNK * len(chunks)], F32, name=f"a_ps{g}") for g, chunks in enumerate(BANKS)]
+
+        def evacuate(g):
+            tag = f"grouped{g + 1}" if g == 2 else f"a_max{g}"
+            a_max.append(sb.tile([P, 1], F32, name=f"a_max{g}", tag=tag, align_bytes=64))
+            nc.vector.tensor_scalar(
+                a_sb[:, g * CHUNK : (g + 1) * CHUNK], a_ps[g][:], 1.0, a_max[g - 1][:] if g else None,
+                ALU.mult, ALU.max, accum_out=a_max[g][:],
+            )
+
+        for g, chunks in enumerate(BANKS):
+            for n, c in enumerate(chunks):
+                grouped = sb.tile([P, CHUNK, PACK], BF16, name=f"voc_grouped{c}", tag=f"grouped{c}", align_bytes=64)
+                interleave(nc.scalar.copy, grouped, voc_raw[c], 0, SCALAR_COLS[c])
+                if SCALAR_COLS[c] < CHUNK:
+                    interleave(nc.vector.tensor_copy, grouped, voc_raw[c], SCALAR_COLS[c], CHUNK)
+                codes, scales = quantize(f"voc{c}", grouped, CHUNK)
+                nc.tensor.matmul_mx(
+                    out=a_ps[g][:, n * CHUNK : (n + 1) * CHUNK], lhsT=ht_codes[:].bitcast(FP8X4), lhsT_scale=ht_scales[:],
+                    rhs=codes[:].bitcast(FP8X4), rhs_scale=scales[:], start=True, stop=True,
+                )
+            if g >= 1:
+                evacuate(g - 1)
+        evacuate(len(BANKS) - 1)
+
+        hd_grouped = late.tile([P, Q, PACK], BF16, name="hd_grouped", offset=3 * chunk_bytes, align_bytes=64)
+        interleave(nc.scalar.copy, hd_grouped, hd_raw, 0, Q)
+        hd_codes, hd_scales = quantize("hd", hd_grouped, Q)
+
+        neg_a_max = sb.tile([P, 1], F32, name="neg_a_max")
+        nc.scalar.mul(neg_a_max[:], a_max[-1][:], -1.0)
+        a_exp = sb.tile([P, V], F32, name="a_exp")
+        z = sb.tile([P, len(BANKS)], F32, name="z")
+        for g, chunks in enumerate(BANKS):
+            nc.scalar.activation(
+                a_exp[:, chunks[0] * CHUNK : (chunks[-1] + 1) * CHUNK], a_ps[g][:], ACT.Exp,
+                bias=neg_a_max[:], accum_out=z[:, g : g + 1],
+            )
+        a_g = late.tile([P, I], F32, name="a_g", offset=3 * chunk_bytes)
+        nc.vector.tensor_copy(a_g[:], a_sb[:].indirect(offs2_sb[:]))
+        z_dw = sb.tile([P, 1], F32, name="z_dw")
+        z_dw_parts = sb.tile([P, len(BANKS)], F32, name="z_dw_parts")
+        nc.scalar.activation(z_dw_parts[:], z[:], ACT.Abs, scale=dw_sb[:], accum_out=z_dw[:])
+        dw_neg = sb.tile([P, 1], F32, name="dw_neg")
+        nc.vector.tensor_scalar(dw_neg[:], dw_sb[:], 0.0, None, ALU.is_lt)
+        target_exp = sb.tile([P, I], F32, name="target_exp")
+        nc.scalar.activation(target_exp[:], a_g[:], ACT.Exp, bias=neg_a_max[:])
+        emb_words_g = sb.tile([P, I], U32, name="emb_words_g", tag="a_then_words", align_bytes=64)
+        emb_word_g = [emb_words_g[:, :HALF], emb_words_g[:, HALF:]]
+        target = sb.tile([P, I], F32, name="target")
+
+        neg_b = sb.tile([P, I], F32, name="neg_b")
+        neg_b_max = [sb.tile([P, 1], F32, name=f"neg_b_max{h}") for h in range(2)]
+        b_ps = [ps.tile([P, HALF], F32, name=f"b_ps{h}") for h in range(2)]
+        for h in range(2):
+            nc.vector.tensor_copy(emb_word_g[h], word_store[:].indirect(offs_sb[:, h * 16 : (h + 1) * 16]))
+            nc.tensor.matmul_mx(
+                out=b_ps[h][:], lhsT=hd_codes[:].bitcast(FP8X4), lhsT_scale=hd_scales[:],
+                rhs=emb_word_g[h].bitcast(FP8X4), rhs_scale=emb_scale_g[:, h * HALF : (h + 1) * HALF],
+                start=True, stop=True,
+            )
+        z_dw_rec = late.tile([P, 1], F32, name="z_dw_rec", offset=store_offset)
+        nc.vector.reciprocal(z_dw_rec[:], z_dw[:])
+        nc.scalar.activation(target[:], target_exp[:], ACT.Identity, bias=dw_neg[:], scale=z_dw_rec[:])
+        for h in range(2):
+            nc.vector.tensor_scalar(
+                neg_b[:, h * HALF : (h + 1) * HALF], b_ps[h][:], -1.0, neg_b_max[0][:] if h else None,
+                ALU.mult, ALU.min, accum_out=neg_b_max[h][:],
+            )
+        draft = sb.tile([P, I], F32, name="draft")
+        draft_sum = sb.tile([P, 1], F32, name="draft_sum")
+        nc.scalar.activation(draft[:], neg_b[:], ACT.Exp, bias=neg_b_max[1][:], scale=-1.0, accum_out=draft_sum[:])
+        u = sb.tile([P, I], F32, name="u")
+        u_sum = sb.tile([P, 1], F32, name="u_sum")
+        nc.vector.scalar_tensor_tensor(u[:], target[:], draft_sum[:], draft[:], ALU.mult, ALU.min, accum_out=u_sum[:])
+        u_rec = sb.tile([P, 1], F32, name="u_rec")
+        nc.vector.reciprocal(u_rec[:], u_sum[:])
+        for h, queue in enumerate((nc.sync, nc.scalar)):
+            y = sb.tile([P, HALF], F32, name=f"y{h}")
+            cols = slice(h * HALF, (h + 1) * HALF)
+            nc.vector.tensor_scalar(y[:], u[:, cols], u_rec[:], 512.0, ALU.mult, ALU.mult)
+            queue.dma_start(out=out[:, cols], in_=y[:])

@@ -18,7 +18,7 @@ D, V, I, T, Q = 512, 1024, 512, 2048, 128
 CHUNK = 256
 HALF = I // 2
 SCALAR_COLS = [160, 160, 160, 96]
-BANKS = [[0], [1], [2], [3]]
+BANKS = [[0], [1, 2], [3]]
 FLOPS = 2 * D * Q * (V + I)
 
 
@@ -52,11 +52,12 @@ def tile_attend_acceptedmass_kernel(tc, ht, hd, voc, emb_words, emb_scales, dw, 
         dw_sb = late.tile([P, 1], F32, name="dw_sb", offset=store_offset + T * 4)
         warm = sb.tile([P, 1], F32, name="warm")
         warm_out = sb.tile([P, 1], F32, name="warm_out")
-        nc.vector.memset(scale_store[:].bitcast(U32), 0)
+        nc.vector.memset(scale_store[:, : T // 2].bitcast(U32), 0)
+        nc.gpsimd.memset(scale_store[:, T // 2 :].bitcast(U32), 0)
         nc.vector.memset(gate[:, 0:1], 0.0)
         nc.vector.tensor_copy(warm[:], gate[:, 0:1])
         nc.scalar.activation(warm_out[:], warm[:], ACT.Exp)
-        a_sb = sb.tile([P, V], F32, name="a_sb", tag="a_then_words", align_bytes=64)
+        a_sb = sb.tile([P, V], F32, name="a_sb")
 
         voc_v = voc.rearrange("(p j) w -> p j w", j=PACK)
         nc.sync.dma_start(offs_sb[:], offs)
@@ -79,7 +80,10 @@ def tile_attend_acceptedmass_kernel(tc, ht, hd, voc, emb_words, emb_scales, dw, 
 
         def quantize(name, grouped, width):
             tag = "scales_then_codes" if name == "voc0" else name + "_codes"
-            codes = sb.tile([P, width], U32, name=name + "_codes", tag=tag, align_bytes=64)
+            if name == "hd":
+                codes = late.tile([P, width], U32, name="hd_codes", offset=2 * chunk_bytes + 2048, align_bytes=64)
+            else:
+                codes = sb.tile([P, width], U32, name=name + "_codes", tag=tag, align_bytes=64)
             scales = sb.tile([P, width], U8, name=name + "_scales", align_bytes=64)
             nc.vector.quantize_mx(
                 out=codes[:].bitcast(FP8X4), scales=scales[:], in_=grouped[:].rearrange("p w j -> p (w j)")
@@ -96,11 +100,21 @@ def tile_attend_acceptedmass_kernel(tc, ht, hd, voc, emb_words, emb_scales, dw, 
         a_ps = [ps.tile([P, CHUNK * len(chunks)], F32, name=f"a_ps{g}") for g, chunks in enumerate(BANKS)]
 
         def evacuate(g):
-            tag = f"grouped{g + 1}" if g == 2 else f"a_max{g}"
-            a_max.append(sb.tile([P, 1], F32, name=f"a_max{g}", tag=tag, align_bytes=64))
+            chunks = BANKS[g]
+            if g < 2:
+                held_by = BANKS[g + 1][0]
+                if g == 0:
+                    first = late.tile([P, 1], F32, name="a_max0", offset=held_by * chunk_bytes + 3072)
+                    a_max.append(first[:])
+                else:
+                    span = late.tile([P, chunk_bytes // 4 + 1], F32, name="a_max1_span", offset=2 * chunk_bytes)
+                    a_max.append(span[:, chunk_bytes // 4 :])
+            else:
+                last = sb.tile([P, 1], F32, name=f"a_max{g}")
+                a_max.append(last[:])
             nc.vector.tensor_scalar(
-                a_sb[:, g * CHUNK : (g + 1) * CHUNK], a_ps[g][:], 1.0, a_max[g - 1][:] if g else None,
-                ALU.mult, ALU.max, accum_out=a_max[g][:],
+                a_sb[:, chunks[0] * CHUNK : (chunks[-1] + 1) * CHUNK], a_ps[g][:], 1.0, a_max[g - 1] if g else None,
+                ALU.mult, ALU.max, accum_out=a_max[g],
             )
 
         for g, chunks in enumerate(BANKS):
@@ -114,54 +128,63 @@ def tile_attend_acceptedmass_kernel(tc, ht, hd, voc, emb_words, emb_scales, dw, 
                     out=a_ps[g][:, n * CHUNK : (n + 1) * CHUNK], lhsT=ht_codes[:].bitcast(FP8X4), lhsT_scale=ht_scales[:],
                     rhs=codes[:].bitcast(FP8X4), rhs_scale=scales[:], start=True, stop=True,
                 )
-            if g >= 1:
-                evacuate(g - 1)
+                if g >= 1 and n == 0:
+                    evacuate(g - 1)
         evacuate(len(BANKS) - 1)
 
-        hd_grouped = late.tile([P, Q, PACK], BF16, name="hd_grouped", offset=3 * chunk_bytes, align_bytes=64)
+        hd_grouped = late.tile([P, Q, PACK], BF16, name="hd_grouped", offset=3 * chunk_bytes + 1024, align_bytes=64)
         interleave(nc.scalar.copy, hd_grouped, hd_raw, 0, Q)
         hd_codes, hd_scales = quantize("hd", hd_grouped, Q)
 
         neg_a_max = sb.tile([P, 1], F32, name="neg_a_max")
-        nc.scalar.mul(neg_a_max[:], a_max[-1][:], -1.0)
+        nc.scalar.mul(neg_a_max[:], a_max[-1], -1.0)
         a_exp = sb.tile([P, V], F32, name="a_exp")
-        z = sb.tile([P, len(BANKS)], F32, name="z")
-        for g, chunks in enumerate(BANKS):
-            nc.scalar.activation(
-                a_exp[:, chunks[0] * CHUNK : (chunks[-1] + 1) * CHUNK], a_ps[g][:], ACT.Exp,
-                bias=neg_a_max[:], accum_out=z[:, g : g + 1],
-            )
-        a_g = late.tile([P, I], F32, name="a_g", offset=3 * chunk_bytes)
-        nc.vector.tensor_copy(a_g[:], a_sb[:].indirect(offs2_sb[:]))
+        z = sb.tile([P, 1], F32, name="z")
+        nc.scalar.activation(a_exp[:], a_sb[:], ACT.Exp, bias=neg_a_max[:], accum_out=z[:])
         z_dw = sb.tile([P, 1], F32, name="z_dw")
-        z_dw_parts = sb.tile([P, len(BANKS)], F32, name="z_dw_parts")
-        nc.scalar.activation(z_dw_parts[:], z[:], ACT.Abs, scale=dw_sb[:], accum_out=z_dw[:])
+        nc.scalar.activation(z_dw[:], z[:], ACT.Abs, scale=dw_sb[:])
         dw_neg = sb.tile([P, 1], F32, name="dw_neg")
-        nc.vector.tensor_scalar(dw_neg[:], dw_sb[:], 0.0, None, ALU.is_lt)
-        target_exp = sb.tile([P, I], F32, name="target_exp")
-        nc.scalar.activation(target_exp[:], a_g[:], ACT.Exp, bias=neg_a_max[:])
-        emb_words_g = sb.tile([P, I], U32, name="emb_words_g", tag="a_then_words", align_bytes=64)
-        emb_word_g = [emb_words_g[:, :HALF], emb_words_g[:, HALF:]]
-        target = sb.tile([P, I], F32, name="target")
+        nc.gpsimd.tensor_scalar(dw_neg[:], dw_sb[:], 0.0, None, ALU.is_lt)
+        minus_one = sb.tile([P, 1], F32, name="minus_one")
+        nc.gpsimd.memset(minus_one[:], -1.0)
+        z_dw_rec = sb.tile([P, 1], F32, name="z_dw_rec")
+        nc.gpsimd.tensor_tensor(z_dw_rec[:], z_dw[:], minus_one[:], ALU.pow)
 
+        halves = [slice(h * HALF, (h + 1) * HALF) for h in range(2)]
+        lists = [slice(h * HALF // 16, (h + 1) * HALF // 16) for h in range(2)]
+        a_g = [sb.tile([P, HALF], F32, name=f"a_g{h}") for h in range(2)]
+        target_exp = sb.tile([P, I], F32, name="target_exp")
+        emb_word_g = [
+            late.tile([P, HALF], U32, name=f"emb_word_g{h}", offset=2 * chunk_bytes + h * HALF * 4, align_bytes=64)
+            for h in range(2)
+        ]
         neg_b = sb.tile([P, I], F32, name="neg_b")
-        neg_b_max = [sb.tile([P, 1], F32, name=f"neg_b_max{h}") for h in range(2)]
+        neg_b_max = [
+            sb.tile([P, 1], F32, name="neg_b_max0", tag="b_max_then_target"),
+            sb.tile([P, 1], F32, name="neg_b_max1"),
+        ]
         b_ps = [ps.tile([P, HALF], F32, name=f"b_ps{h}") for h in range(2)]
+
+        def look_up_a(h):
+            nc.vector.tensor_copy(a_g[h][:], a_sb[:].indirect(offs2_sb[:, lists[h]]))
+            nc.scalar.activation(target_exp[:, halves[h]], a_g[h][:], ACT.Exp, bias=neg_a_max[:])
+
+        look_up_a(0)
         for h in range(2):
-            nc.vector.tensor_copy(emb_word_g[h], word_store[:].indirect(offs_sb[:, h * 16 : (h + 1) * 16]))
+            nc.vector.tensor_copy(emb_word_g[h][:], word_store[:].indirect(offs_sb[:, lists[h]]))
             nc.tensor.matmul_mx(
                 out=b_ps[h][:], lhsT=hd_codes[:].bitcast(FP8X4), lhsT_scale=hd_scales[:],
-                rhs=emb_word_g[h].bitcast(FP8X4), rhs_scale=emb_scale_g[:, h * HALF : (h + 1) * HALF],
+                rhs=emb_word_g[h][:].bitcast(FP8X4), rhs_scale=emb_scale_g[:, halves[h]],
                 start=True, stop=True,
             )
-        z_dw_rec = late.tile([P, 1], F32, name="z_dw_rec", offset=store_offset)
-        nc.vector.reciprocal(z_dw_rec[:], z_dw[:])
-        nc.scalar.activation(target[:], target_exp[:], ACT.Identity, bias=dw_neg[:], scale=z_dw_rec[:])
+        look_up_a(1)
         for h in range(2):
             nc.vector.tensor_scalar(
                 neg_b[:, h * HALF : (h + 1) * HALF], b_ps[h][:], -1.0, neg_b_max[0][:] if h else None,
                 ALU.mult, ALU.min, accum_out=neg_b_max[h][:],
             )
+        target = sb.tile([P, I], F32, name="target", tag="b_max_then_target")
+        nc.vector.tensor_scalar(target[:], target_exp[:], z_dw_rec[:], dw_neg[:], ALU.mult, ALU.add)
         draft = sb.tile([P, I], F32, name="draft")
         draft_sum = sb.tile([P, 1], F32, name="draft_sum")
         nc.scalar.activation(draft[:], neg_b[:], ACT.Exp, bias=neg_b_max[1][:], scale=-1.0, accum_out=draft_sum[:])

@@ -42,41 +42,35 @@ def tile_attend_acceptedmass_kernel(tc, ht, hd, voc, emb_words, emb_scales, dw, 
         scale_store = sb.tile([P, T], U8, name="scale_store", tag="scales_then_codes", align_bytes=64)
         ht_raw = sb.tile([P, PACK, Q], F32, name="ht_raw")
         chunk_bytes = PACK * CHUNK * 4
-        late_bytes = 4 * chunk_bytes + PACK * Q * 4 + T * 4 + 32
-        gate = late.tile([P, late_bytes // 4], F32, name="gate", offset=0)
         voc_raw = [late.tile([P, PACK, CHUNK], F32, name=f"voc_raw{c}", offset=c * chunk_bytes) for c in range(n_chunks)]
-        hd_raw = late.tile([P, PACK, Q], F32, name="hd_raw", offset=4 * chunk_bytes)
-        store_offset = 4 * chunk_bytes + PACK * Q * 4
-        word_store = late.tile([P, T], U32, name="word_store", offset=store_offset)
+        hd_raw = sb.tile([P, PACK, Q], F32, name="hd_raw")
+        word_store = sb.tile([P, T], U32, name="word_store")
+        dw_sb = sb.tile([P, 1], F32, name="dw_sb")
+        emb_plane = sb.tile([P, I], U8, name="emb_plane", align_bytes=64)
 
-        dw_sb = late.tile([P, 1], F32, name="dw_sb", offset=store_offset + T * 4)
         warm = sb.tile([P, 1], F32, name="warm")
         warm_out = sb.tile([P, 1], F32, name="warm_out")
-        nc.vector.memset(scale_store[:, : T // 2].bitcast(U32), 0)
-        nc.gpsimd.memset(scale_store[:, T // 2 :].bitcast(U32), 0)
-        nc.vector.memset(gate[:, 0:1], 0.0)
-        nc.vector.tensor_copy(warm[:], gate[:, 0:1])
+        nc.vector.memset(warm[:], 0.0)
         nc.scalar.activation(warm_out[:], warm[:], ACT.Exp)
+        nc.vector.memset(scale_store[0:16, :].bitcast(I32), 0)
+        nc.vector.memset(scale_store[64:128, :].bitcast(I32), 0)
+        nc.gpsimd.memset(scale_store[32:64, :].bitcast(I32), 0)
+        nc.gpsimd.memset(emb_plane[:].bitcast(I32), 0)
         a_sb = sb.tile([P, V], F32, name="a_sb")
 
         voc_v = voc.rearrange("(p j) w -> p j w", j=PACK)
         nc.sync.dma_start(offs_sb[:], offs)
+        nc.sync.dma_start(out=scale_store[16:32, :].bitcast(I32), in_=emb_scales[0].bitcast(I32))
         nc.sync.dma_start(out=ht_raw[:], in_=ht.rearrange("(p j) w -> p j w", j=PACK))
-        for g in range(4):
-            nc.sync.dma_start(
-                out=scale_store[32 * g : 32 * g + 4, :].bitcast(I32),
-                in_=emb_scales[0, 4 * g : 4 * g + 4, :].bitcast(I32),
-            )
+        nc.sync.dma_start(offs2_sb[:], offs2)
         for c in range(n_chunks):
             nc.sync.dma_start(out=voc_raw[c][:], in_=voc_v[:, :, c * CHUNK : (c + 1) * CHUNK])
         nc.sync.dma_start(out=hd_raw[:], in_=hd.rearrange("(p j) w -> p j w", j=PACK))
-        nc.sync.dma_start(out=dw_sb[:], in_=dw)
         nc.sync.dma_start(
             out=word_store[:].bitcast(I32),
             in_=emb_words[0].rearrange("p n t -> p (n t)").bitcast(I32),
         )
-
-        nc.sync.dma_start(offs2_sb[:], offs2)
+        nc.sync.dma_start(out=dw_sb[:], in_=dw)
 
         def quantize(name, grouped, width):
             tag = "scales_then_codes" if name == "voc0" else name + "_codes"
@@ -95,6 +89,11 @@ def tile_attend_acceptedmass_kernel(tc, ht, hd, voc, emb_words, emb_scales, dw, 
         ht_codes, ht_scales = quantize("ht", ht_grouped, Q)
         emb_scale_g = sb.tile([P, I], U8, name="emb_scale_g", align_bytes=64)
         nc.vector.tensor_copy(emb_scale_g[:], scale_store[:].indirect(offs_sb[:]))
+        for g in range(4):
+            nc.scalar.dma_start(
+                out=emb_plane[32 * g : 32 * g + 4, :].bitcast(I32),
+                in_=emb_scale_g[16 + 4 * g : 20 + 4 * g, :].bitcast(I32),
+            )
 
         a_max = []
         a_ps = [ps.tile([P, CHUNK * len(chunks)], F32, name=f"a_ps{g}") for g, chunks in enumerate(BANKS)]
@@ -174,7 +173,7 @@ def tile_attend_acceptedmass_kernel(tc, ht, hd, voc, emb_words, emb_scales, dw, 
             nc.vector.tensor_copy(emb_word_g[h][:], word_store[:].indirect(offs_sb[:, lists[h]]))
             nc.tensor.matmul_mx(
                 out=b_ps[h][:], lhsT=hd_codes[:].bitcast(FP8X4), lhsT_scale=hd_scales[:],
-                rhs=emb_word_g[h][:].bitcast(FP8X4), rhs_scale=emb_scale_g[:, halves[h]],
+                rhs=emb_word_g[h][:].bitcast(FP8X4), rhs_scale=emb_plane[:, halves[h]],
                 start=True, stop=True,
             )
         look_up_a(1)

from contextlib import ExitStack

import concourse.mybir as mybir

F32 = mybir.dt.float32
BF16 = mybir.dt.bfloat16
I32 = mybir.dt.int32
U32 = mybir.dt.uint32
U16 = mybir.dt.uint16
U8 = mybir.dt.uint8
FP8X4 = mybir.dt.float8_e4m3fn_x4
ALU = mybir.AluOpType
ACT = mybir.ActivationFunctionType

P = 128
PACK = 4
D, V, I, T, Q = 512, 1024, 512, 2048, 128
CHUNK = 256
HALF = I // 2
SCALAR_COLS = [160, 160, 160, 96]
BANKS = [[0], [1, 2], [3]]
FLOPS = 2 * D * Q * (V + I)


def interleave(engine_copy, grouped, raw, c0, c1):
    engine_copy(
        out=grouped[:, c0:c1, :].rearrange("p (c i) t -> p c t i", i=4),
        in_=raw[:, :, c0:c1].rearrange("p t (c i) -> p c t i", i=4),
    )


def tile_attend_acceptedmass_kernel(tc, ht, hd, voc, emb_words, emb_scales, dw, offs, offs2, out):
    nc = tc.nc
    n_chunks = V // CHUNK
    with ExitStack() as ctx:
        sb = ctx.enter_context(tc.tile_pool(name="sb", bufs=1))
        late = ctx.enter_context(tc.tile_pool(name="late", bufs=1))
        ps = ctx.enter_context(tc.psum_pool(name="ps", bufs=1))

        offs_sb = sb.tile([P, I // 16], U16, name="offs_sb")
        offs2_sb = sb.tile([P, I // 16], U16, name="offs2_sb")
        scale_store = sb.tile([P, T], U8, name="scale_store", tag="scales_then_codes", align_bytes=64)
        ht_raw = sb.tile([P, PACK, Q], F32, name="ht_raw")
        chunk_bytes = PACK * CHUNK * 4
        voc_raw = [late.tile([P, PACK, CHUNK], F32, name=f"voc_raw{c}", offset=c * chunk_bytes) for c in range(n_chunks)]
        hd_raw = sb.tile([P, PACK, Q], F32, name="hd_raw")
        word_store = sb.tile([P, T], U32, name="word_store")
        dw_sb = sb.tile([P, 1], F32, name="dw_sb")
        emb_plane = sb.tile([P, I], U8, name="emb_plane", align_bytes=64)

        warm = sb.tile([P, 1], F32, name="warm")
        warm_out = sb.tile([P, 1], F32, name="warm_out")
        nc.vector.memset(warm[:], 0.0)
        nc.scalar.activation(warm_out[:], warm[:], ACT.Exp)
        nc.vector.memset(scale_store[0:16, :].bitcast(I32), 0)
        nc.vector.memset(scale_store[64:128, :].bitcast(I32), 0)
        nc.gpsimd.memset(scale_store[32:64, :].bitcast(I32), 0)
        nc.gpsimd.memset(emb_plane[:].bitcast(I32), 0)
        a_sb = sb.tile([P, V], F32, name="a_sb")

        voc_v = voc.rearrange("(p j) w -> p j w", j=PACK)
        nc.sync.dma_start(offs_sb[:], offs)
        nc.sync.dma_start(out=scale_store[16:32, :].bitcast(I32), in_=emb_scales[0].bitcast(I32))
        nc.sync.dma_start(out=ht_raw[:], in_=ht.rearrange("(p j) w -> p j w", j=PACK))
        nc.sync.dma_start(offs2_sb[:], offs2)
        for c in range(n_chunks):
            nc.sync.dma_start(out=voc_raw[c][:], in_=voc_v[:, :, c * CHUNK : (c + 1) * CHUNK])
        nc.sync.dma_start(out=hd_raw[:], in_=hd.rearrange("(p j) w -> p j w", j=PACK))
        nc.sync.dma_start(
            out=word_store[:].bitcast(I32),
            in_=emb_words[0].rearrange("p n t -> p (n t)").bitcast(I32),
        )
        nc.sync.dma_start(out=dw_sb[:], in_=dw)

        def quantize(name, grouped, width):
            tag = "scales_then_codes" if name == "voc0" else name + "_codes"
            if name == "hd":
                codes = late.tile([P, width], U32, name="hd_codes", offset=2 * chunk_bytes + 2048, align_bytes=64)
            else:
                codes = sb.tile([P, width], U32, name=name + "_codes", tag=tag, align_bytes=64)
            scales = sb.tile([P, width], U8, name=name + "_scales", align_bytes=64)
            nc.vector.quantize_mx(
                out=codes[:].bitcast(FP8X4), scales=scales[:], in_=grouped[:].rearrange("p w j -> p (w j)")
            )
            return codes, scales

        ht_grouped = sb.tile([P, Q, PACK], BF16, name="ht_grouped", align_bytes=64)
        interleave(nc.scalar.copy, ht_grouped, ht_raw, 0, Q)
        ht_codes, ht_scales = quantize("ht", ht_grouped, Q)
        emb_scale_g = sb.tile([P, I], U8, name="emb_scale_g", align_bytes=64)
        nc.vector.tensor_copy(emb_scale_g[:], scale_store[:].indirect(offs_sb[:]))
        for g in range(4):
            nc.scalar.dma_start(
                out=emb_plane[32 * g : 32 * g + 4, :].bitcast(I32),
                in_=emb_scale_g[16 + 4 * g : 20 + 4 * g, :].bitcast(I32),
            )

        a_max = []
        a_ps = [ps.tile([P, CHUNK * len(chunks)], F32, name=f"a_ps{g}") for g, chunks in enumerate(BANKS)]

        def evacuate(g):
            chunks = BANKS[g]
            if g < 2:
                held_by = BANKS[g + 1][0]
                if g == 0:
                    first = late.tile([P, 1], F32, name="a_max0", offset=held_by * chunk_bytes + 3072)
                    a_max.append(first[:])
                else:
                    span = late.tile([P, chunk_bytes // 4 + 1], F32, name="a_max1_span", offset=2 * chunk_bytes)
                    a_max.append(span[:, chunk_bytes // 4 :])
            else:
                last = sb.tile([P, 1], F32, name=f"a_max{g}")
                a_max.append(last[:])
            nc.vector.tensor_scalar(
                a_sb[:, chunks[0] * CHUNK : (chunks[-1] + 1) * CHUNK], a_ps[g][:], 1.0, a_max[g - 1] if g else None,
                ALU.mult, ALU.max, accum_out=a_max[g],
            )

        for g, chunks in enumerate(BANKS):
            for n, c in enumerate(chunks):
                grouped = sb.tile([P, CHUNK, PACK], BF16, name=f"voc_grouped{c}", tag=f"grouped{c}", align_bytes=64)
                interleave(nc.scalar.copy, grouped, voc_raw[c], 0, SCALAR_COLS[c])
                if SCALAR_COLS[c] < CHUNK:
                    interleave(nc.vector.tensor_copy, grouped, voc_raw[c], SCALAR_COLS[c], CHUNK)
                codes, scales = quantize(f"voc{c}", grouped, CHUNK)
                nc.tensor.matmul_mx(
                    out=a_ps[g][:, n * CHUNK : (n + 1) * CHUNK], lhsT=ht_codes[:].bitcast(FP8X4), lhsT_scale=ht_scales[:],
                    rhs=codes[:].bitcast(FP8X4), rhs_scale=scales[:], start=True, stop=True,
                )
                if g >= 1 and n == 0:
                    evacuate(g - 1)
        evacuate(len(BANKS) - 1)

        hd_grouped = late.tile([P, Q, PACK], BF16, name="hd_grouped", offset=3 * chunk_bytes + 1024, align_bytes=64)
        interleave(nc.scalar.copy, hd_grouped, hd_raw, 0, Q)
        hd_codes, hd_scales = quantize("hd", hd_grouped, Q)

        neg_a_max = sb.tile([P, 1], F32, name="neg_a_max")
        nc.scalar.mul(neg_a_max[:], a_max[-1], -1.0)
        a_exp = sb.tile([P, V], F32, name="a_exp")
        z = sb.tile([P, 1], F32, name="z")
        nc.scalar.activation(a_exp[:], a_sb[:], ACT.Exp, bias=neg_a_max[:], accum_out=z[:])
        z_dw = sb.tile([P, 1], F32, name="z_dw")
        nc.scalar.activation(z_dw[:], z[:], ACT.Abs, scale=dw_sb[:])
        dw_neg = sb.tile([P, 1], F32, name="dw_neg")
        nc.gpsimd.tensor_scalar(dw_neg[:], dw_sb[:], 0.0, None, ALU.is_lt)
        minus_one = sb.tile([P, 1], F32, name="minus_one")
        nc.gpsimd.memset(minus_one[:], -1.0)
        z_dw_rec = sb.tile([P, 1], F32, name="z_dw_rec")
        nc.gpsimd.tensor_tensor(z_dw_rec[:], z_dw[:], minus_one[:], ALU.pow)

        halves = [slice(h * HALF, (h + 1) * HALF) for h in range(2)]
        lists = [slice(h * HALF // 16, (h + 1) * HALF // 16) for h in range(2)]
        a_g = [sb.tile([P, HALF], F32, name=f"a_g{h}") for h in range(2)]
        target_exp = sb.tile([P, I], F32, name="target_exp")
        emb_word_g = [
            late.tile([P, HALF], U32, name=f"emb_word_g{h}", offset=2 * chunk_bytes + h * HALF * 4, align_bytes=64)
            for h in range(2)
        ]
        neg_b = sb.tile([P, I], F32, name="neg_b")
        neg_b_max = [
            sb.tile([P, 1], F32, name="neg_b_max0", tag="b_max_then_target"),
            sb.tile([P, 1], F32, name="neg_b_max1"),
        ]
        b_ps = [ps.tile([P, HALF], F32, name=f"b_ps{h}") for h in range(2)]

        def look_up_a(h):
            nc.vector.tensor_copy(a_g[h][:], a_sb[:].indirect(offs2_sb[:, lists[h]]))
            nc.scalar.activation(target_exp[:, halves[h]], a_g[h][:], ACT.Exp, bias=neg_a_max[:])

        look_up_a(0)
        for h in range(2):
            nc.vector.tensor_copy(emb_word_g[h][:], word_store[:].indirect(offs_sb[:, lists[h]]))
            nc.tensor.matmul_mx(
                out=b_ps[h][:], lhsT=hd_codes[:].bitcast(FP8X4), lhsT_scale=hd_scales[:],
                rhs=emb_word_g[h][:].bitcast(FP8X4), rhs_scale=emb_plane[:, halves[h]],
                start=True, stop=True,
            )
        look_up_a(1)
        for h in range(2):
            nc.vector.tensor_scalar(
                neg_b[:, h * HALF : (h + 1) * HALF], b_ps[h][:], -1.0, neg_b_max[0][:] if h else None,
                ALU.mult, ALU.min, accum_out=neg_b_max[h][:],
            )
        target = sb.tile([P, I], F32, name="target", tag="b_max_then_target")
        nc.vector.tensor_scalar(target[:], target_exp[:], z_dw_rec[:], dw_neg[:], ALU.mult, ALU.add)
        draft = sb.tile([P, I], F32, name="draft")
        draft_sum = sb.tile([P, 1], F32, name="draft_sum")
        nc.scalar.activation(draft[:], neg_b[:], ACT.Exp, bias=neg_b_max[1][:], scale=-1.0, accum_out=draft_sum[:])
        u = sb.tile([P, I], F32, name="u")
        u_sum = sb.tile([P, 1], F32, name="u_sum")
        nc.vector.scalar_tensor_tensor(u[:], target[:], draft_sum[:], draft[:], ALU.mult, ALU.min, accum_out=u_sum[:])
        u_rec = sb.tile([P, 1], F32, name="u_rec")
        nc.vector.reciprocal(u_rec[:], u_sum[:])
        for h, queue in enumerate((nc.sync, nc.scalar)):
            y = sb.tile([P, HALF], F32, name=f"y{h}")
            cols = slice(h * HALF, (h + 1) * HALF)
            nc.vector.tensor_scalar(y[:], u[:, cols], u_rec[:], 512.0, ALU.mult, ALU.mult)
            queue.dma_start(out=out[:, cols], in_=y[:])
